import numpy as np
import ml_dtypes


def mxq(x, axis, fmt="e4m3"):
    dtype, down = {"e4m3": (ml_dtypes.float8_e4m3fn, 7), "e5m2": (ml_dtypes.float8_e5m2, 14)}[fmt]
    v = np.moveaxis(np.asarray(x, np.float32).astype(ml_dtypes.bfloat16).astype(np.float64), axis, -1)
    blocks = v.reshape(v.shape[:-1] + (-1, 32))
    amax = np.abs(blocks).max(-1, keepdims=True)
    byte = np.maximum(np.where(amax > 0, np.frexp(amax)[1] - 1 + 127, 0) - down, 1)
    scale = np.exp2(byte - 127.0)
    codes = (blocks / scale).astype(np.float32).astype(dtype).astype(np.float64)
    return np.moveaxis((codes * scale).reshape(v.shape), -1, axis)


WIDE = False


def mx_kscale(k):
    if not WIDE:
        return np.ones(k)
    levels = np.array([10, -10, 5, -5, 0])
    if k % 512:
        return np.exp2(np.random.permutation(np.resize(levels, k // 32))).repeat(32)
    a = np.empty((k // 512, 16))
    for p in range(k // 512):
        a[p, :8] = np.random.permutation(np.resize(levels, 8))
        for g in range(8):
            far = levels[np.abs(levels - a[p, g]) >= 10]
            a[p, g + 8] = far[np.random.randint(len(far))]
    return np.exp2(a.ravel()).repeat(32)


def f64(x):
    return np.asarray(x).astype(np.float64)


def striped(idx):
    return np.tile(idx.reshape(-1, 16).T, (8, 1)).astype(np.uint16)


def unstriped(offs):
    return offs[:16].T.reshape(-1).astype(np.int64)


E2M1 = np.array([0.0, 0.5, 1.0, 1.5, 2.0, 3.0, 4.0, 6.0, -0.0, -0.5, -1.0, -1.5, -2.0, -3.0, -4.0, -6.0])


def pack_weight(w, fmt):
    k, n = w.shape
    w = f64(np.asarray(w, np.float32).astype(ml_dtypes.bfloat16)).reshape(k // 32, 32, n)
    amax = np.abs(w).max(1)
    if fmt == "e4m3":
        byte = np.frexp(amax)[1] - 1 + 127 - 7
    else:
        mant, ex = np.frexp(amax / 6.0)
        byte = np.where(mant > 0.5, ex, ex - 1) + 127
    byte = np.clip(np.where(amax > 0, byte, 1), 1, 254)
    scaled = (w * np.exp2(127.0 - byte)[:, None, :]).reshape(k, n).astype(np.float32)
    by_word = np.ascontiguousarray(scaled.reshape(k // 512, 128, 4, n).transpose(0, 1, 3, 2))
    if fmt == "e4m3":
        words = by_word.astype(ml_dtypes.float8_e4m3fn).view(np.uint8)
    else:
        c = by_word.astype(ml_dtypes.float4_e2m1fn).view(np.uint8) & 0xF
        words = (c[..., 0::2] | (c[..., 1::2] << 4)).reshape(k // 512, 128, 2 * n)
    return np.ascontiguousarray(words), np.ascontiguousarray(byte.astype(np.uint8).reshape(k // 512, 16, n))


def unpack_weight(words, scales, fmt):
    g, _, n = scales.shape
    words = np.ascontiguousarray(words).reshape(g, 128, n, -1)
    if fmt == "e4m3":
        vals = words.view(ml_dtypes.float8_e4m3fn).astype(np.float64)
    else:
        nib = np.empty((g, 128, n, 4), np.uint8)
        nib[..., 0::2] = words & 0xF
        nib[..., 1::2] = words >> 4
        vals = E2M1[nib]
    vals = vals * np.repeat(np.exp2(scales.astype(np.float64) - 127.0), 8, axis=1)[..., None]
    return vals.transpose(0, 1, 3, 2).reshape(g * 512, n)


def gelu(v):
    return 0.5 * v * (1.0 + np.tanh(np.sqrt(2.0 / np.pi) * (v + 0.044715 * v**3)))


K, T, E, C, H, N = 1536, 512, 6, 256, 512, 128
TOP = 3


def by_expert(wq, xq):
    return np.concatenate([wq[e].T @ xq[:, e * C:(e + 1) * C] for e in range(E)], axis=1)


def setup_inputs():
    n = np.random.standard_normal
    s = mx_kscale(K)[:, None]
    u = mx_kscale(H)
    deal = np.repeat(np.arange(E), C).reshape(TOP, T)[:, np.random.permutation(T)]
    deal = np.take_along_axis(deal, np.argsort(np.random.rand(TOP, T), axis=0), axis=0)
    for _ in range(8):
        s_, t_ = np.random.permutation(T).reshape(2, -1); r = np.random.randint(TOP, size=T // 2); x, y = deal[r, s_].copy(), deal[r, t_].copy()
        ok = ~((deal[:, s_] == y).any(0) | (deal[:, t_] == x).any(0)); deal[r[ok], s_[ok]] = y[ok]; deal[r[ok], t_[ok]] = x[ok]
    order = np.lexsort((np.random.rand(TOP * T), deal.reshape(-1)))
    slot_token = order % T; pos = np.empty(TOP * T, np.int64); pos[order] = np.arange(TOP * T); pos = pos.reshape(TOP, T)
    g = np.random.uniform(0.5, 1.5, (TOP, T)); g = g / g.sum(0)
    w1 = [pack_weight(m, "e2m1") for m in n((E + 1, K, H)) / np.sqrt(K) / s[None] * u[None, None, :]]
    w2 = [pack_weight(m, "e2m1") for m in n((E + 1, H, N)) / np.sqrt(H) / u[None, :, None]]
    return {
        "xT": (n((K, T)) * s).astype(np.float32),
        "w1_words": np.stack([m[0] for m in w1]),
        "w1_scales": np.stack([m[1] for m in w1]),
        "w2_words": np.stack([m[0] for m in w2]),
        "w2_scales": np.stack([m[1] for m in w2]),
        "gate": np.stack([np.tile(r, (N, 1)) for r in g]).astype(np.float32),
        "offs": striped(slot_token),
        "pos1": striped(pos[0]),
        "pos2": striped(pos[1]),
        "pos3": striped(pos[2]),
    }


def reference(xT, w1_words, w1_scales, w2_words, w2_scales, gate, offs, pos1, pos2, pos3):
    idx = unstriped(offs)
    w1 = np.stack([unpack_weight(w1_words[e], w1_scales[e], "e2m1") for e in range(E + 1)])
    w2 = np.stack([unpack_weight(w2_words[e], w2_scales[e], "e2m1") for e in range(E + 1)])
    w1q, w2q = w1, w2
    xs = mxq(f64(xT), 0, "e4m3")
    hs = gelu(w1q[E].T @ xs)
    ys = w2q[E].T @ mxq(hs, 0, "e4m3")
    xq = mxq(f64(xT)[:, idx], 0, "e4m3")
    h = gelu(by_expert(w1q, xq))
    y = by_expert(w2q, mxq(h, 0, "e4m3"))
    return ys + sum(f64(gate[r]) * y[:, unstriped(p)] for r, p in enumerate((pos1, pos2, pos3)))

@@ -1,0 +1,221 @@
+from contextlib import ExitStack
+
+import concourse.mybir as mybir
+from concourse.masks import make_identity
+
+K, T, E, C, H, N = 1536, 512, 6, 256, 512, 128
+TOP = 3
+SLOTS = E * C
+FLOPS = 2 * (SLOTS + T) * (K * H + H * N)
+
+F32 = mybir.dt.float32
+BF16 = mybir.dt.bfloat16
+I32 = mybir.dt.int32
+U32 = mybir.dt.uint32
+U16 = mybir.dt.uint16
+U8 = mybir.dt.uint8
+FP8X4 = mybir.dt.float8_e4m3fn_x4
+FP4X4 = mybir.dt.float4_e2m1fn_x4
+GELU = mybir.ActivationFunctionType.Gelu_apprx_tanh
+MULT = mybir.AluOpType.mult
+ADD = mybir.AluOpType.add
+
+P = 128
+PASSES = K // 512
+WIN = 704
+GROUPS = (512, 256, 256, 256, 128, 128)
+GATHER_RING = 4
+EARLY = 2
+
+
+def tile_moe_shr_mlp_gelu_kernel(
+    tc, xT, w1_words, w1_scales, w2_words, w2_scales, gate, offs, pos1, pos2, pos3, out
+):
+    nc = tc.nc
+    with ExitStack() as ctx:
+        lists = ctx.enter_context(tc.tile_pool(name="lists", bufs=1))
+        sb = ctx.enter_context(tc.tile_pool(name="sb", bufs=1))
+        ps = ctx.enter_context(tc.psum_pool(name="ps", bufs=1))
+
+        def tile(name, shape, dtype, tag=None):
+            return sb.tile(shape, dtype, name=name, tag=tag or name, align_bytes=64)
+
+        offs_t = lists.tile([P, SLOTS // 16], U16, name="offs_t")
+        pos_t = [lists.tile([P, T // 16], U16, name="pos_t%d" % r) for r in range(TOP)]
+
+        raw = [tile("raw%d" % j, [P, 2 * T], F32) for j in range(2 * PASSES)]
+        win = [tile("win%d" % s, [P, 2 * 2 * WIN], BF16) for s in range(PASSES)]
+        sc_early = tile("sc_early", [P, EARLY * PASSES, H], U8)
+        sc_late = tile("sc_late", [P, (E + 1 - EARLY) * PASSES, H], U8)
+        w2 = tile("w2", [P, E + 1, 2 * N], U8)
+        sc2 = tile("sc2", [P, E + 1, N], U8)
+        ident = tile("ident", [P, P], F32)
+        warm = tile("warm", [P, 8], F32)
+        warm2 = tile("warm2", [P, 8], F32)
+
+        nc.vector.memset(sc_early[:].bitcast(I32), 0)
+        nc.vector.memset(warm[:], 0.0)
+        nc.scalar.activation(warm2[:], warm[:], GELU)
+        for s in range(PASSES):
+            for u in range(2):
+                nc.vector.memset(win[s][:, 2 * (u * WIN + T) : 2 * (u + 1) * WIN], 0.0)
+        nc.gpsimd.memset(sc2[:].bitcast(I32), 0)
+        nc.gpsimd.memset(sc_late[:].bitcast(I32), 0)
+        make_identity(nc, ident[:])
+
+        def load_scales(plane, src):
+            rows = src.rearrange("e s (q r) i -> r q (e s) i", r=4)
+            for r in range(4):
+                nc.sync.dma_start(plane[r:P:32, :, :].bitcast(I32), rows[r].bitcast(I32))
+
+        w1 = {}
+
+        def load_w1(lo, hi, tag=None):
+            words = tile("w1_%d" % lo, [P, (hi - lo) * PASSES, 2 * H], U8, tag)
+            nc.sync.dma_start(words[:].bitcast(I32), w1_words[lo:hi].rearrange("e s p b -> p (e s) b").bitcast(I32))
+            for e in range(lo, hi):
+                w1[e] = words[:, (e - lo) * PASSES : (e - lo + 1) * PASSES, :]
+
+        x_rows = xT.rearrange("(s p u d) t -> s u p (d t)", s=PASSES, u=2, d=2)
+        nc.sync.dma_start(raw[0][:], x_rows[0, 0])
+        nc.sync.dma_start(offs_t[:], offs)
+        for j in range(1, 2 * PASSES):
+            nc.sync.dma_start(raw[j][:], x_rows[j // 2, j % 2])
+        load_w1(0, 1)
+        load_scales(sc_early, w1_scales[0:EARLY])
+        load_w1(1, 2)
+        load_scales(sc2, w2_scales)
+        load_scales(sc_late, w1_scales[EARLY : E + 1])
+        nc.sync.dma_start(w2[:].bitcast(I32), w2_words.rearrange("e s p b -> p (e s) b").bitcast(I32))
+        for r, pos in enumerate((pos1, pos2, pos3)):
+            nc.sync.dma_start(pos_t[r][:], pos)
+
+        for j in range(2 * PASSES):
+            s, u = divmod(j, 2)
+            pairs = win[s][:, 2 * u * WIN : 2 * (u * WIN + T)].rearrange("p (t d) -> p t d", d=2)
+            rows = raw[j][:].rearrange("p (d t) -> p t d", d=2)
+            if j == 0:
+                nc.vector.tensor_copy(pairs, rows)
+            else:
+                nc.scalar.copy(pairs, rows)
+
+        load_w1(2, 4, "raw0")
+        load_w1(4, 6, "raw1")
+        load_w1(6, 7, "raw2")
+        gate_t = tile("gate_t", [P, TOP, T], F32, "raw3")
+        nc.sync.dma_start(gate_t[:], gate.rearrange("r p t -> p r t"))
+
+        gathered = [tile("gathered%d" % i, [P, 2 * T], U32) for i in range(GATHER_RING)]
+        woven = [raw[5], raw[4], tile("woven", [P, 2 * T], F32)]
+        shared_woven = tile("shared_woven", [P, 4 * T], U32)
+        a_banks = [ps.tile([P, H], F32, name="a_bank%d" % i) for i in range(4)]
+        t_banks = [ps.tile([P, 4 * P], F32, name="t_bank%d" % i) for i in range(2)]
+        y_banks = [ps.tile([P, 2 * C], F32, name="y_bank%d" % i) for i in range(2)]
+        h_rows = [tile("h_rows%d" % i, [P, H], BF16) for i in range(4)]
+        h_cols = [tile("h_cols%d" % i, [P, 4 * C], BF16) for i in range(2)]
+        y_all = tile("y_all", [P, SLOTS], F32)
+
+        def quantise(name, values, width):
+            codes = tile("codes_" + name, [P, width], U32)
+            scales = tile("scales_" + name, [P, width], U8)
+            nc.vector.quantize_mx(out=codes[:].bitcast(FP8X4), scales=scales[:], in_=values)
+            return codes, scales
+
+        def first_layer(s, e, block, codes, scales, col):
+            plane = sc_early[:, e * PASSES + s, :] if e < EARLY else sc_late[:, (e - EARLY) * PASSES + s, :]
+            nc.tensor.matmul_mx(
+                out=a_banks[block % 4][:],
+                lhsT=codes[:, col : col + P].bitcast(FP8X4),
+                lhsT_scale=scales[:, col : col + P],
+                rhs=w1[e][:, s, :].bitcast(FP4X4),
+                rhs_scale=plane,
+                start=(s == 0),
+                stop=(s == PASSES - 1),
+            )
+
+        def second_layer(e, chunk, blocks, y_out):
+            width = len(blocks) * P
+            turned = t_banks[chunk % 2]
+            for b, block in enumerate(blocks):
+                rows = h_rows[block % 4]
+                nc.scalar.activation(
+                    rows[:].rearrange("p (u m d) -> p u m d", u=2, d=2),
+                    a_banks[block % 4][:].rearrange("p (m u d) -> p u m d", u=2, d=2),
+                    GELU,
+                )
+                for u in range(2):
+                    nc.tensor.transpose(
+                        turned[:, (2 * b + u) * P : (2 * b + u + 1) * P],
+                        rows[:].bitcast(F32)[:, u * P : (u + 1) * P],
+                        ident[:],
+                    )
+            cols = h_cols[chunk % 2][:, 0 : 4 * width]
+            nc.scalar.copy(
+                cols.bitcast(F32).rearrange("p (b t u) -> p b t u", t=P, u=2),
+                turned[:, 0 : 2 * width].rearrange("p (b u t) -> p b t u", u=2, t=P),
+            )
+            codes, scales = quantise("h%d" % chunk, cols, width)
+            nc.tensor.matmul_mx(
+                out=y_out,
+                lhsT=w2[:, e, :].bitcast(FP4X4),
+                lhsT_scale=sc2[:, e, :],
+                rhs=codes[:].bitcast(FP8X4),
+                rhs_scale=scales[:],
+                start=True,
+                stop=True,
+            )
+
+        unit = 0
+        chunk = 0
+        first = 0
+        for g, size in enumerate(GROUPS):
+            blocks = range(first // P, (first + size) // P)
+            for s in range(PASSES):
+                planes = gathered[unit % GATHER_RING][:, 0 : 2 * size]
+                for u in range(2):
+                    window = win[s][:].bitcast(U32)[:, u * WIN : (u + 1) * WIN]
+                    nc.vector.tensor_copy(
+                        planes[:, u * size : (u + 1) * size],
+                        window.indirect(offs_t[:, first // 16 : (first + size) // 16]),
+                    )
+                if g == len(GROUPS) - 1 and s == PASSES - 1:
+                    words = shared_woven[:, 2 * T - size : 2 * T + size]
+                else:
+                    words = woven[unit % len(woven)][:].bitcast(U32)[:, 0 : 2 * size]
+                nc.scalar.copy(words.rearrange("p (c u) -> p c u", u=2), planes.rearrange("p (u c) -> p c u", u=2))
+                codes, scales = quantise("x%d" % unit, words.bitcast(BF16), size)
+                for block in blocks:
+                    first_layer(s, block * P // C, block, codes, scales, block * P - first)
+                unit = unit + 1
+            for lo in range(first, first + size, C):
+                width = min(C, size)
+                y_bank = y_banks[chunk % 2][:, 0:width]
+                second_layer(lo // C, chunk, range(lo // P, (lo + width) // P), y_bank)
+                nc.scalar.copy(y_all[:, lo : lo + width], y_bank)
+                chunk = chunk + 1
+            first = first + size
+
+        blocks = range(SLOTS // P, (SLOTS + T) // P)
+        for s in range(PASSES):
+            words = shared_woven[:, (s % 2) * 2 * T : (s % 2 + 1) * 2 * T]
+            nc.vector.tensor_copy(
+                words.bitcast(F32).rearrange("p (c u) -> p c u", u=2),
+                win[s][:].bitcast(F32).rearrange("p (u c) -> p c u", u=2)[:, 0:T, :],
+            )
+            codes, scales = quantise("xs%d" % s, words.bitcast(BF16), T)
+            for block in blocks:
+                first_layer(s, E, block, codes, scales, block * P - SLOTS)
+        ys = y_banks[chunk % 2]
+
+        picked = [tile("picked%d" % r, [P, T], F32) for r in range(TOP)]
+        for r in range(TOP):
+            nc.vector.tensor_tensor(picked[r][:], y_all[:].indirect(pos_t[r][:]), gate_t[:, r, :], MULT)
+        for half in range(2):
+            second_layer(E, chunk + half, blocks[2 * half : 2 * half + 2], ys[:, half * C : (half + 1) * C])
+        sum2 = tile("sum2", [P, T], F32)
+        sum3 = tile("sum3", [P, T], F32)
+        total = tile("total", [P, T], F32)
+        nc.vector.tensor_tensor(sum2[:], picked[0][:], picked[1][:], ADD)
+        nc.vector.tensor_tensor(sum3[:], sum2[:], picked[2][:], ADD)
+        nc.vector.tensor_tensor(total[:], sum3[:], ys[:], ADD)
+        nc.sync.dma_start(out, total[:])

@@ -22,7 +22,7 @@ ADD = mybir.AluOpType.add
 
 P = 128
 PASSES = K // 512
-WIN = 704
+WIN = 512
 GROUPS = (512, 256, 256, 256, 128, 128)
 GATHER_RING = 4
 EARLY = 2
@@ -45,23 +45,21 @@ def tile_moe_shr_mlp_gelu_kernel(
 
         raw = [tile("raw%d" % j, [P, 2 * T], F32) for j in range(2 * PASSES)]
         win = [tile("win%d" % s, [P, 2 * 2 * WIN], BF16) for s in range(PASSES)]
-        sc_early = tile("sc_early", [P, EARLY * PASSES, H], U8)
-        sc_late = tile("sc_late", [P, (E + 1 - EARLY) * PASSES, H], U8)
+        sc1 = {lo: tile("sc1_%d" % lo, [P, (hi - lo) * PASSES, H], U8) for lo, hi in ((0, 2), (2, 4), (4, 6), (6, 7))}
+        plane_of = {e: sc1[lo][:, (e - lo) * PASSES : (e - lo + 1) * PASSES, :] for lo, hi in ((0, 2), (2, 4), (4, 6), (6, 7)) for e in range(lo, hi)}
         w2 = tile("w2", [P, E + 1, 2 * N], U8)
         sc2 = tile("sc2", [P, E + 1, N], U8)
         ident = tile("ident", [P, P], F32)
         warm = tile("warm", [P, 8], F32)
         warm2 = tile("warm2", [P, 8], F32)
 
-        nc.vector.memset(sc_early[:].bitcast(I32), 0)
+        nc.vector.memset(sc1[0][:].bitcast(I32), 0)
         nc.vector.memset(warm[:], 0.0)
         nc.scalar.activation(warm2[:], warm[:], GELU)
-        for s in range(PASSES):
-            for u in range(2):
-                nc.vector.memset(win[s][:, 2 * (u * WIN + T) : 2 * (u + 1) * WIN], 0.0)
-        nc.gpsimd.memset(sc2[:].bitcast(I32), 0)
-        nc.gpsimd.memset(sc_late[:].bitcast(I32), 0)
         make_identity(nc, ident[:])
+        for lo in list(sc1)[1:]:
+            (nc.vector if lo < 4 else nc.gpsimd).memset(sc1[lo][:].bitcast(I32), 0)
+        nc.gpsimd.memset(sc2[:].bitcast(I32), 0)
 
         def load_scales(plane, src):
             rows = src.rearrange("e s (q r) i -> r q (e s) i", r=4)
@@ -70,9 +68,9 @@ def tile_moe_shr_mlp_gelu_kernel(
 
         w1 = {}
 
-        def load_w1(lo, hi, tag=None):
+        def load_w1(lo, hi, tag=None, queue=nc.sync):
             words = tile("w1_%d" % lo, [P, (hi - lo) * PASSES, 2 * H], U8, tag)
-            nc.sync.dma_start(words[:].bitcast(I32), w1_words[lo:hi].rearrange("e s p b -> p (e s) b").bitcast(I32))
+            queue.dma_start(words[:].bitcast(I32), w1_words[lo:hi].rearrange("e s p b -> p (e s) b").bitcast(I32))
             for e in range(lo, hi):
                 w1[e] = words[:, (e - lo) * PASSES : (e - lo + 1) * PASSES, :]
 
@@ -81,14 +79,6 @@ def tile_moe_shr_mlp_gelu_kernel(
         nc.sync.dma_start(offs_t[:], offs)
         for j in range(1, 2 * PASSES):
             nc.sync.dma_start(raw[j][:], x_rows[j // 2, j % 2])
-        load_w1(0, 1)
-        load_scales(sc_early, w1_scales[0:EARLY])
-        load_w1(1, 2)
-        load_scales(sc2, w2_scales)
-        load_scales(sc_late, w1_scales[EARLY : E + 1])
-        nc.sync.dma_start(w2[:].bitcast(I32), w2_words.rearrange("e s p b -> p (e s) b").bitcast(I32))
-        for r, pos in enumerate((pos1, pos2, pos3)):
-            nc.sync.dma_start(pos_t[r][:], pos)
 
         for j in range(2 * PASSES):
             s, u = divmod(j, 2)
@@ -99,45 +89,51 @@ def tile_moe_shr_mlp_gelu_kernel(
             else:
                 nc.scalar.copy(pairs, rows)
 
-        load_w1(2, 4, "raw0")
-        load_w1(4, 6, "raw1")
-        load_w1(6, 7, "raw2")
-        gate_t = tile("gate_t", [P, TOP, T], F32, "raw3")
+        load_w1(0, 2)
+        load_scales(sc1[0], w1_scales[0:2])
+        load_w1(2, 4)
+        load_scales(sc1[2], w1_scales[2:4])
+        nc.sync.dma_start(w2[:].bitcast(I32), w2_words.rearrange("e s p b -> p (e s) b").bitcast(I32))
+        load_scales(sc2, w2_scales)
+        load_w1(4, 6)
+        load_scales(sc1[4], w1_scales[4:6])
+        load_w1(6, 7)
+        load_scales(sc1[6], w1_scales[6:7])
+        for r, pos in enumerate((pos1, pos2, pos3)):
+            nc.sync.dma_start(pos_t[r][:], pos)
+        gate_t = tile("gate_t", [P, TOP, T], F32)
         nc.sync.dma_start(gate_t[:], gate.rearrange("r p t -> p r t"))
 
-        gathered = [tile("gathered%d" % i, [P, 2 * T], U32) for i in range(GATHER_RING)]
-        woven = [raw[5], raw[4], tile("woven", [P, 2 * T], F32)]
-        shared_woven = tile("shared_woven", [P, 4 * T], U32)
         a_banks = [ps.tile([P, H], F32, name="a_bank%d" % i) for i in range(4)]
         t_banks = [ps.tile([P, 4 * P], F32, name="t_bank%d" % i) for i in range(2)]
         y_banks = [ps.tile([P, 2 * C], F32, name="y_bank%d" % i) for i in range(2)]
-        h_rows = [tile("h_rows%d" % i, [P, H], BF16) for i in range(4)]
+        h_rows = [tile("h_rows%d" % i, [P, 4 * C], BF16) for i in range(16)]
         h_cols = [tile("h_cols%d" % i, [P, 4 * C], BF16) for i in range(2)]
+        late_cols = tile("late_cols", [P, 4 * C], BF16)
         y_all = tile("y_all", [P, SLOTS], F32)
 
-        def quantise(name, values, width):
-            codes = tile("codes_" + name, [P, width], U32)
-            scales = tile("scales_" + name, [P, width], U8)
+        def quantise(name, values, width, tag=None, scale_tag=None):
+            codes = tile("codes_" + name, [P, width], U32, tag)
+            scales = tile("scales_" + name, [P, width], U8, scale_tag)
             nc.vector.quantize_mx(out=codes[:].bitcast(FP8X4), scales=scales[:], in_=values)
             return codes, scales
 
         def first_layer(s, e, block, codes, scales, col):
-            plane = sc_early[:, e * PASSES + s, :] if e < EARLY else sc_late[:, (e - EARLY) * PASSES + s, :]
             nc.tensor.matmul_mx(
                 out=a_banks[block % 4][:],
                 lhsT=codes[:, col : col + P].bitcast(FP8X4),
                 lhsT_scale=scales[:, col : col + P],
                 rhs=w1[e][:, s, :].bitcast(FP4X4),
-                rhs_scale=plane,
+                rhs_scale=plane_of[e][:, s, :],
                 start=(s == 0),
                 stop=(s == PASSES - 1),
             )
 
-        def second_layer(e, chunk, blocks, y_out):
-            width = len(blocks) * P
-            turned = t_banks[chunk % 2]
-            for b, block in enumerate(blocks):
-                rows = h_rows[block % 4]
+        def activate(chunk):
+            lo, size = chunks[chunk]
+            for b in range(size // P):
+                block = lo // P + b
+                rows = h_rows[block][:, 0:H]
                 nc.scalar.activation(
                     rows[:].rearrange("p (u m d) -> p u m d", u=2, d=2),
                     a_banks[block % 4][:].rearrange("p (m u d) -> p u m d", u=2, d=2),
@@ -145,16 +141,20 @@ def tile_moe_shr_mlp_gelu_kernel(
                 )
                 for u in range(2):
                     nc.tensor.transpose(
-                        turned[:, (2 * b + u) * P : (2 * b + u + 1) * P],
+                        t_banks[chunk % 2][:, (2 * b + u) * P : (2 * b + u + 1) * P],
                         rows[:].bitcast(F32)[:, u * P : (u + 1) * P],
                         ident[:],
                     )
-            cols = h_cols[chunk % 2][:, 0 : 4 * width]
+
+        def second_layer(chunk, cols, y_out):
+            lo, size = chunks[chunk]
+            e = min(lo // C, E)
+            cols = cols[:, 0 : 4 * size]
             nc.scalar.copy(
                 cols.bitcast(F32).rearrange("p (b t u) -> p b t u", t=P, u=2),
-                turned[:, 0 : 2 * width].rearrange("p (b u t) -> p b t u", u=2, t=P),
+                t_banks[chunk % 2][:, 0 : 2 * size].rearrange("p (b u t) -> p b t u", u=2, t=P),
             )
-            codes, scales = quantise("h%d" % chunk, cols, width)
+            codes, scales = quantise("h%d" % chunk, cols, size)
             nc.tensor.matmul_mx(
                 out=y_out,
                 lhsT=w2[:, e, :].bitcast(FP4X4),
@@ -165,57 +165,86 @@ def tile_moe_shr_mlp_gelu_kernel(
                 stop=True,
             )
 
-        unit = 0
-        chunk = 0
-        first = 0
-        for g, size in enumerate(GROUPS):
-            blocks = range(first // P, (first + size) // P)
-            for s in range(PASSES):
-                planes = gathered[unit % GATHER_RING][:, 0 : 2 * size]
+        routed = [(e * C, C) for e in range(E - 0)] + [(b * P, P) for b in range(2 * (E - 0), 2 * E)]
+        chunks = routed + [(SLOTS, C), (SLOTS + C, C)]
+        units = [(c, s) for s in range(PASSES) for c in range(EARLY)]
+        units = units + [(c, s) for c in range(EARLY, len(routed)) for s in range(PASSES)]
+        last = len(units) - 1
+        done_at = {c: units.index((c, PASSES - 1)) for c in range(len(routed))}
+        gathered = {}
+        for n in range(len(units)):
+            if n < 6:
+                gathered[n] = tile("gathered%d" % n, [P, 2 * C], U32)
+            else:
+                gathered[n] = gathered[1 if n == 6 else n - 2]
+
+        shared_words = {}
+
+        def weave_shared(copy, dtype, s, tag):
+            words = tile("shared%d" % s, [P, 2 * T], dtype, tag) if tag else raw[5][:].bitcast(dtype)
+            copy(
+                words[:].rearrange("p (c u) -> p c u", u=2),
+                win[s][:].bitcast(dtype).rearrange("p (u c) -> p c u", u=2),
+            )
+            shared_words[s] = words
+
+        shared_behind = {}
+
+        for n in range(len(units) + 6):
+            if n < len(units):
+                c, s = units[n]
+                lo, size = chunks[c]
+                planes = gathered[n][:, 0 : 2 * size]
                 for u in range(2):
-                    window = win[s][:].bitcast(U32)[:, u * WIN : (u + 1) * WIN]
                     nc.vector.tensor_copy(
                         planes[:, u * size : (u + 1) * size],
-                        window.indirect(offs_t[:, first // 16 : (first + size) // 16]),
+                        win[s][:].bitcast(U32)[:, u * T : (u + 1) * T].indirect(offs_t[:, lo // 16 : (lo + size) // 16]),
                     )
-                if g == len(GROUPS) - 1 and s == PASSES - 1:
-                    words = shared_woven[:, 2 * T - size : 2 * T + size]
-                else:
-                    words = woven[unit % len(woven)][:].bitcast(U32)[:, 0 : 2 * size]
-                nc.scalar.copy(words.rearrange("p (c u) -> p c u", u=2), planes.rearrange("p (u c) -> p c u", u=2))
-                codes, scales = quantise("x%d" % unit, words.bitcast(BF16), size)
-                for block in blocks:
-                    first_layer(s, block * P // C, block, codes, scales, block * P - first)
-                unit = unit + 1
-            for lo in range(first, first + size, C):
-                width = min(C, size)
-                y_bank = y_banks[chunk % 2][:, 0:width]
-                second_layer(lo // C, chunk, range(lo // P, (lo + width) // P), y_bank)
-                nc.scalar.copy(y_all[:, lo : lo + width], y_bank)
-                chunk = chunk + 1
-            first = first + size
+                woven = raw[5 - n % 4 // 2][:].bitcast(U32)[:, (n % 2) * 2 * C : (n % 2) * 2 * C + 2 * size]
+                for done in range(2):
+                    if n == done_at[done] + 3:
+                        woven = h_rows[2 * done + 0][:].bitcast(U32)
+                nc.scalar.copy(woven.rearrange("p (c u) -> p c u", u=2), planes.rearrange("p (u c) -> p c u", u=2))
+            for done in done_at:
+                if n == done_at[done] + 2:
+                    activate(done)
+            if n < len(units):
+                codes, scales = quantise("x%d" % n, woven.bitcast(BF16), size)
+                for b in range(size // P):
+                    first_layer(s, lo // C, lo // P + b, codes, scales, b * P)
+            for done in done_at:
+                y_bank = y_banks[done % 2][:, 0 : chunks[done][1]]
+                if n == done_at[done] + (3+1 if done == 0 else 3):
+                    second_layer(done, late_cols if done == len(routed) - 1 else h_cols[done % 2], y_bank)
+                if n == done_at[done] + 6:
+                    nc.scalar.copy(y_all[:, chunks[done][0] : sum(chunks[done])], y_bank)
+            if n - 3 in shared_behind:
+                weave_shared(nc.scalar.copy, U32, shared_behind[n - 3], "codes_x%d" % (n - 3))
 
-        blocks = range(SLOTS // P, (SLOTS + T) // P)
         for s in range(PASSES):
-            words = shared_woven[:, (s % 2) * 2 * T : (s % 2 + 1) * 2 * T]
-            nc.vector.tensor_copy(
-                words.bitcast(F32).rearrange("p (c u) -> p c u", u=2),
-                win[s][:].bitcast(F32).rearrange("p (u c) -> p c u", u=2)[:, 0:T, :],
-            )
-            codes, scales = quantise("xs%d" % s, words.bitcast(BF16), T)
-            for block in blocks:
-                first_layer(s, E, block, codes, scales, block * P - SLOTS)
-        ys = y_banks[chunk % 2]
+            if s not in shared_words:
+                weave_shared(nc.vector.tensor_copy, I32, s, (None, "codes_x%d" % last, "late_cols")[s])
+        for s, tag, scale_tag in ((0, None, None), (1, None, None), (2, None, None)):
+            codes, scales = quantise("xs%d" % s, shared_words[s][:].bitcast(BF16), T, tag, scale_tag)
+            for b in range(T // P):
+                first_layer(s, E, SLOTS // P + b, codes, scales, b * P)
+        ys = y_banks[len(routed) % 2]
 
         picked = [tile("picked%d" % r, [P, T], F32) for r in range(TOP)]
         for r in range(TOP):
             nc.vector.tensor_tensor(picked[r][:], y_all[:].indirect(pos_t[r][:]), gate_t[:, r, :], MULT)
+        shared_cols = [h_cols[0], tile("shared_cols", [P, 4 * C], BF16)]
         for half in range(2):
-            second_layer(E, chunk + half, blocks[2 * half : 2 * half + 2], ys[:, half * C : (half + 1) * C])
-        sum2 = tile("sum2", [P, T], F32)
+            activate(len(routed) + half)
+            second_layer(len(routed) + half, shared_cols[half], ys[:, half * C : (half + 1) * C])
+        sum2 = tile("sum2", [P, T], F32, "shared_cols")
         sum3 = tile("sum3", [P, T], F32)
         total = tile("total", [P, T], F32)
-        nc.vector.tensor_tensor(sum2[:], picked[0][:], picked[1][:], ADD)
-        nc.vector.tensor_tensor(sum3[:], sum2[:], picked[2][:], ADD)
-        nc.vector.tensor_tensor(total[:], sum3[:], ys[:], ADD)
-        nc.sync.dma_start(out, total[:])
+        halves = [slice(0, C), slice(C, T)]
+        for cols in halves:
+            nc.vector.tensor_tensor(sum2[:, cols], picked[0][:, cols], picked[1][:, cols], ADD)
+        for cols in halves:
+            nc.vector.tensor_tensor(sum3[:, cols], sum2[:, cols], picked[2][:, cols], ADD)
+        for cols in halves:
+            nc.vector.tensor_tensor(total[:, cols], sum3[:, cols], ys[:, cols], ADD)
+            nc.sync.dma_start(out[:, cols], total[:, cols])

@@ -22,10 +22,14 @@ ADD = mybir.AluOpType.add
 
 P = 128
 PASSES = K // 512
-WIN = 512
-GROUPS = (512, 256, 256, 256, 128, 128)
-GATHER_RING = 4
-EARLY = 2
+PIECES = 2 * PASSES
+FIRST = 2
+DEFERRED = 4
+SCALE_GROUPS = ((0, 2), (2, 4), (4, 7))
+GELU_AFTER = 2
+TURN_AFTER = 3
+KEEP_AFTER = 5
+REUSE_AFTER = 4
 
 
 def tile_moe_shr_mlp_gelu_kernel(
@@ -37,68 +41,66 @@ def tile_moe_shr_mlp_gelu_kernel(
         sb = ctx.enter_context(tc.tile_pool(name="sb", bufs=1))
         ps = ctx.enter_context(tc.psum_pool(name="ps", bufs=1))
 
-        def tile(name, shape, dtype, tag=None):
-            return sb.tile(shape, dtype, name=name, tag=tag or name, align_bytes=64)
+        def tile(name, shape, dtype, after=None):
+            return sb.tile(shape, dtype, name=name, tag=after or name, align_bytes=64)
 
         offs_t = lists.tile([P, SLOTS // 16], U16, name="offs_t")
         pos_t = [lists.tile([P, T // 16], U16, name="pos_t%d" % r) for r in range(TOP)]
 
-        raw = [tile("raw%d" % j, [P, 2 * T], F32) for j in range(2 * PASSES)]
-        win = [tile("win%d" % s, [P, 2 * 2 * WIN], BF16) for s in range(PASSES)]
-        sc1 = {lo: tile("sc1_%d" % lo, [P, (hi - lo) * PASSES, H], U8) for lo, hi in ((0, 2), (2, 4), (4, 6), (6, 7))}
-        plane_of = {e: sc1[lo][:, (e - lo) * PASSES : (e - lo + 1) * PASSES, :] for lo, hi in ((0, 2), (2, 4), (4, 6), (6, 7)) for e in range(lo, hi)}
+        raw = [tile("raw%d" % j, [P, 2 * T], F32) for j in range(PIECES)]
+        pairs = [tile("pairs%d" % s, [P, 4 * T], BF16) for s in range(PASSES)]
+        w1_planes = {lo: tile("w1_planes%d" % lo, [P, (hi - lo) * PASSES, H], U8) for lo, hi in SCALE_GROUPS}
         w2 = tile("w2", [P, E + 1, 2 * N], U8)
-        sc2 = tile("sc2", [P, E + 1, N], U8)
+        w2_planes = tile("w2_planes", [P, E + 1, N], U8)
         ident = tile("ident", [P, P], F32)
-        warm = tile("warm", [P, 8], F32)
-        warm2 = tile("warm2", [P, 8], F32)
+        warm_in = tile("warm_in", [P, 8], F32)
+        warm_out = tile("warm_out", [P, 8], F32)
 
-        nc.vector.memset(sc1[0][:].bitcast(I32), 0)
-        nc.vector.memset(warm[:], 0.0)
-        nc.scalar.activation(warm2[:], warm[:], GELU)
+        nc.vector.memset(w1_planes[0][:].bitcast(I32), 0)
+        nc.vector.memset(warm_in[:], 0.0)
+        nc.scalar.activation(warm_out[:], warm_in[:], GELU)
         make_identity(nc, ident[:])
-        for lo in list(sc1)[1:]:
-            (nc.vector if lo < 4 else nc.gpsimd).memset(sc1[lo][:].bitcast(I32), 0)
-        nc.gpsimd.memset(sc2[:].bitcast(I32), 0)
-
-        def load_scales(plane, src):
-            rows = src.rearrange("e s (q r) i -> r q (e s) i", r=4)
-            for r in range(4):
-                nc.sync.dma_start(plane[r:P:32, :, :].bitcast(I32), rows[r].bitcast(I32))
-
-        w1 = {}
-
-        def load_w1(lo, hi, tag=None, queue=nc.sync):
-            words = tile("w1_%d" % lo, [P, (hi - lo) * PASSES, 2 * H], U8, tag)
-            queue.dma_start(words[:].bitcast(I32), w1_words[lo:hi].rearrange("e s p b -> p (e s) b").bitcast(I32))
-            for e in range(lo, hi):
-                w1[e] = words[:, (e - lo) * PASSES : (e - lo + 1) * PASSES, :]
+        nc.vector.memset(w1_planes[2][:].bitcast(I32), 0)
+        nc.gpsimd.memset(w1_planes[4][:].bitcast(I32), 0)
+        nc.gpsimd.memset(w2_planes[:].bitcast(I32), 0)
 
         x_rows = xT.rearrange("(s p u d) t -> s u p (d t)", s=PASSES, u=2, d=2)
         nc.sync.dma_start(raw[0][:], x_rows[0, 0])
         nc.sync.dma_start(offs_t[:], offs)
-        for j in range(1, 2 * PASSES):
+        for j in range(1, PIECES):
             nc.sync.dma_start(raw[j][:], x_rows[j // 2, j % 2])
 
-        for j in range(2 * PASSES):
+        for j in range(PIECES):
             s, u = divmod(j, 2)
-            pairs = win[s][:, 2 * u * WIN : 2 * (u * WIN + T)].rearrange("p (t d) -> p t d", d=2)
+            rounded = pairs[s][:, 2 * u * T : 2 * (u + 1) * T].rearrange("p (t d) -> p t d", d=2)
             rows = raw[j][:].rearrange("p (d t) -> p t d", d=2)
             if j == 0:
-                nc.vector.tensor_copy(pairs, rows)
+                nc.vector.tensor_copy(rounded, rows)
             else:
-                nc.scalar.copy(pairs, rows)
+                nc.scalar.copy(rounded, rows)
 
-        load_w1(0, 2)
-        load_scales(sc1[0], w1_scales[0:2])
-        load_w1(2, 4)
-        load_scales(sc1[2], w1_scales[2:4])
+        def load_scales(planes, src):
+            rows = src.rearrange("e s (q r) i -> r q (e s) i", r=4)
+            for r in range(4):
+                nc.sync.dma_start(planes[r:P:32, :, :].bitcast(I32), rows[r].bitcast(I32))
+
+        w1 = {}
+
+        def load_w1(lo, hi):
+            words = tile("w1_%d" % lo, [P, (hi - lo) * PASSES, 2 * H], U8)
+            nc.sync.dma_start(words[:].bitcast(I32), w1_words[lo:hi].rearrange("e s p b -> p (e s) b").bitcast(I32))
+            for e in range(lo, hi):
+                w1[e] = words[:, (e - lo) * PASSES : (e - lo + 1) * PASSES, :]
+
+        w1_plane = {}
+        for lo, hi in SCALE_GROUPS:
+            load_w1(lo, min(hi, E))
+            load_scales(w1_planes[lo], w1_scales[lo:hi])
+            for e in range(lo, hi):
+                w1_plane[e] = w1_planes[lo][:, (e - lo) * PASSES : (e - lo + 1) * PASSES, :]
         nc.sync.dma_start(w2[:].bitcast(I32), w2_words.rearrange("e s p b -> p (e s) b").bitcast(I32))
-        load_scales(sc2, w2_scales)
-        load_w1(4, 6)
-        load_scales(sc1[4], w1_scales[4:6])
-        load_w1(6, 7)
-        load_scales(sc1[6], w1_scales[6:7])
+        load_scales(w2_planes, w2_scales)
+        load_w1(E, E + 1)
         for r, pos in enumerate((pos1, pos2, pos3)):
             nc.sync.dma_start(pos_t[r][:], pos)
         gate_t = tile("gate_t", [P, TOP, T], F32)
@@ -107,14 +109,14 @@ def tile_moe_shr_mlp_gelu_kernel(
         a_banks = [ps.tile([P, H], F32, name="a_bank%d" % i) for i in range(4)]
         t_banks = [ps.tile([P, 4 * P], F32, name="t_bank%d" % i) for i in range(2)]
         y_banks = [ps.tile([P, 2 * C], F32, name="y_bank%d" % i) for i in range(2)]
-        h_rows = [tile("h_rows%d" % i, [P, 4 * C], BF16) for i in range(16)]
-        h_cols = [tile("h_cols%d" % i, [P, 4 * C], BF16) for i in range(2)]
-        late_cols = tile("late_cols", [P, 4 * C], BF16)
+        h_rows = [tile("h_rows%d" % i, [P, 4 * C], BF16) for i in range((SLOTS + T) // P)]
+        h_cols = tile("h_cols", [P, 4 * C], BF16)
+        last_cols = tile("last_cols", [P, 4 * C], BF16)
         y_all = tile("y_all", [P, SLOTS], F32)
 
-        def quantise(name, values, width, tag=None, scale_tag=None):
-            codes = tile("codes_" + name, [P, width], U32, tag)
-            scales = tile("scales_" + name, [P, width], U8, scale_tag)
+        def quantise(name, values, width, after=None):
+            codes = tile("codes_" + name, [P, width], U32, after)
+            scales = tile("scales_" + name, [P, width], U8)
             nc.vector.quantize_mx(out=codes[:].bitcast(FP8X4), scales=scales[:], in_=values)
             return codes, scales
 
@@ -124,119 +126,132 @@ def tile_moe_shr_mlp_gelu_kernel(
                 lhsT=codes[:, col : col + P].bitcast(FP8X4),
                 lhsT_scale=scales[:, col : col + P],
                 rhs=w1[e][:, s, :].bitcast(FP4X4),
-                rhs_scale=plane_of[e][:, s, :],
+                rhs_scale=w1_plane[e][:, s, :],
                 start=(s == 0),
                 stop=(s == PASSES - 1),
             )
 
         def activate(chunk):
-            lo, size = chunks[chunk]
-            for b in range(size // P):
-                block = lo // P + b
+            for b in range(2):
+                block = 2 * chunk + b
                 rows = h_rows[block][:, 0:H]
                 nc.scalar.activation(
-                    rows[:].rearrange("p (u m d) -> p u m d", u=2, d=2),
+                    rows.rearrange("p (u m d) -> p u m d", u=2, d=2),
                     a_banks[block % 4][:].rearrange("p (m u d) -> p u m d", u=2, d=2),
                     GELU,
                 )
                 for u in range(2):
                     nc.tensor.transpose(
                         t_banks[chunk % 2][:, (2 * b + u) * P : (2 * b + u + 1) * P],
-                        rows[:].bitcast(F32)[:, u * P : (u + 1) * P],
+                        rows.bitcast(F32)[:, u * P : (u + 1) * P],
                         ident[:],
                     )
 
-        def second_layer(chunk, cols, y_out):
-            lo, size = chunks[chunk]
-            e = min(lo // C, E)
-            cols = cols[:, 0 : 4 * size]
+        def turn_out(chunk, cols):
             nc.scalar.copy(
                 cols.bitcast(F32).rearrange("p (b t u) -> p b t u", t=P, u=2),
-                t_banks[chunk % 2][:, 0 : 2 * size].rearrange("p (b u t) -> p b t u", u=2, t=P),
+                t_banks[chunk % 2][:].rearrange("p (b u t) -> p b t u", u=2, t=P),
             )
-            codes, scales = quantise("h%d" % chunk, cols, size)
+
+        def project(e, codes, scales, y_out):
             nc.tensor.matmul_mx(
                 out=y_out,
                 lhsT=w2[:, e, :].bitcast(FP4X4),
-                lhsT_scale=sc2[:, e, :],
-                rhs=codes[:].bitcast(FP8X4),
-                rhs_scale=scales[:],
+                lhsT_scale=w2_planes[:, e, :],
+                rhs=codes.bitcast(FP8X4),
+                rhs_scale=scales,
                 start=True,
                 stop=True,
             )
 
-        routed = [(e * C, C) for e in range(E - 0)] + [(b * P, P) for b in range(2 * (E - 0), 2 * E)]
-        chunks = routed + [(SLOTS, C), (SLOTS + C, C)]
-        units = [(c, s) for s in range(PASSES) for c in range(EARLY)]
-        units = units + [(c, s) for c in range(EARLY, len(routed)) for s in range(PASSES)]
-        last = len(units) - 1
-        done_at = {c: units.index((c, PASSES - 1)) for c in range(len(routed))}
-        gathered = {}
-        for n in range(len(units)):
-            if n < 6:
-                gathered[n] = tile("gathered%d" % n, [P, 2 * C], U32)
+        def second_layer(chunk, cols, y_out):
+            turn_out(chunk, cols[:])
+            codes, scales = quantise("h%d" % chunk, cols[:], C)
+            project(min(chunk, E), codes[:], scales[:], y_out)
+
+        deferred_cols = tile("deferred_cols", [P, DEFERRED * 4 * C], BF16)
+        last_woven = tile("last_woven", [P, 2 * C], U32)
+
+        steps = [(e, s) for s in range(PASSES) for e in range(FIRST)]
+        steps = steps + [(e, s) for e in range(FIRST, E) for s in range(PASSES)]
+        last = len(steps) - 1
+        done_at = {e: steps.index((e, PASSES - 1)) for e in range(E)}
+
+        gathered = []
+        for n in range(len(steps)):
+            if n < FIRST * PASSES:
+                gathered.append(tile("gathered%d" % n, [P, 2 * C], U32))
             else:
-                gathered[n] = gathered[1 if n == 6 else n - 2]
+                gathered.append(gathered[1 if n == FIRST * PASSES else n - 2])
 
-        shared_words = {}
+        def woven_buffer(n):
+            for e in range(FIRST):
+                if n == done_at[e] + REUSE_AFTER:
+                    return h_rows[2 * e][:].bitcast(U32)
+            if n == last:
+                return last_woven[:]
+            return raw[PIECES - 1 - n % 4 // 2][:].bitcast(U32)[:, (n % 2) * 2 * C : (n % 2 + 1) * 2 * C]
 
-        def weave_shared(copy, dtype, s, tag):
-            words = tile("shared%d" % s, [P, 2 * T], dtype, tag) if tag else raw[5][:].bitcast(dtype)
-            copy(
-                words[:].rearrange("p (c u) -> p c u", u=2),
-                win[s][:].bitcast(dtype).rearrange("p (u c) -> p c u", u=2),
-            )
-            shared_words[s] = words
-
-        shared_behind = {}
-
-        for n in range(len(units) + 6):
-            if n < len(units):
-                c, s = units[n]
-                lo, size = chunks[c]
-                planes = gathered[n][:, 0 : 2 * size]
+        for n in range(len(steps) + KEEP_AFTER):
+            if n <= last:
+                e, s = steps[n]
                 for u in range(2):
+                    window = pairs[s][:].bitcast(U32)[:, u * T : (u + 1) * T]
                     nc.vector.tensor_copy(
-                        planes[:, u * size : (u + 1) * size],
-                        win[s][:].bitcast(U32)[:, u * T : (u + 1) * T].indirect(offs_t[:, lo // 16 : (lo + size) // 16]),
+                        gathered[n][:, u * C : (u + 1) * C],
+                        window.indirect(offs_t[:, e * C // 16 : (e + 1) * C // 16]),
                     )
-                woven = raw[5 - n % 4 // 2][:].bitcast(U32)[:, (n % 2) * 2 * C : (n % 2) * 2 * C + 2 * size]
-                for done in range(2):
-                    if n == done_at[done] + 3:
-                        woven = h_rows[2 * done + 0][:].bitcast(U32)
-                nc.scalar.copy(woven.rearrange("p (c u) -> p c u", u=2), planes.rearrange("p (u c) -> p c u", u=2))
-            for done in done_at:
-                if n == done_at[done] + 2:
+                woven = woven_buffer(n)
+                nc.scalar.copy(woven.rearrange("p (c u) -> p c u", u=2), gathered[n][:].rearrange("p (u c) -> p c u", u=2))
+            for done in range(E):
+                if n == done_at[done] + GELU_AFTER:
                     activate(done)
-            if n < len(units):
-                codes, scales = quantise("x%d" % n, woven.bitcast(BF16), size)
-                for b in range(size // P):
-                    first_layer(s, lo // C, lo // P + b, codes, scales, b * P)
-            for done in done_at:
-                y_bank = y_banks[done % 2][:, 0 : chunks[done][1]]
-                if n == done_at[done] + (3+1 if done == 0 else 3):
-                    second_layer(done, late_cols if done == len(routed) - 1 else h_cols[done % 2], y_bank)
-                if n == done_at[done] + 6:
-                    nc.scalar.copy(y_all[:, chunks[done][0] : sum(chunks[done])], y_bank)
-            if n - 3 in shared_behind:
-                weave_shared(nc.scalar.copy, U32, shared_behind[n - 3], "codes_x%d" % (n - 3))
+            if n <= last:
+                codes, scales = quantise("x%d" % n, woven.bitcast(BF16), C)
+                for b in range(2):
+                    first_layer(s, e, 2 * e + b, codes, scales, b * P)
+            for done in range(E):
+                turn_at = done_at[max(done, FIRST - 1)] + TURN_AFTER
+                if done < DEFERRED:
+                    if n == turn_at:
+                        turn_out(done, deferred_cols[:, done * 4 * C : (done + 1) * 4 * C])
+                    continue
+                y_bank = t_banks[done % 2][:, 0:C]
+                if n == turn_at:
+                    second_layer(done, last_cols if done == E - 1 else h_cols, y_bank)
+                if n == done_at[done] + KEEP_AFTER:
+                    nc.scalar.copy(y_all[:, done * C : (done + 1) * C], y_bank)
+            if n == last + TURN_AFTER:
+                codes, scales = quantise("deferred", deferred_cols[:], DEFERRED * C, "last_woven")
+                for bank in range(DEFERRED // 2):
+                    for d in (2 * bank, 2 * bank + 1):
+                        cols = slice(d * C, (d + 1) * C)
+                        project(d, codes[:, cols], scales[:, cols], y_banks[bank][:, (d % 2) * C : (d % 2 + 1) * C])
+                    nc.scalar.copy(y_all[:, 2 * bank * C : (2 * bank + 2) * C], y_banks[bank][:])
 
+        shared_woven = []
+        for s, after in enumerate(("codes_x%d" % last, "scales_x%d" % last, "last_cols")):
+            words = tile("shared%d" % s, [P, 2 * T], I32, after)
+            nc.vector.tensor_copy(
+                words[:].rearrange("p (c u) -> p c u", u=2),
+                pairs[s][:].bitcast(I32).rearrange("p (u c) -> p c u", u=2),
+            )
+            shared_woven.append(words)
         for s in range(PASSES):
-            if s not in shared_words:
-                weave_shared(nc.vector.tensor_copy, I32, s, (None, "codes_x%d" % last, "late_cols")[s])
-        for s, tag, scale_tag in ((0, None, None), (1, None, None), (2, None, None)):
-            codes, scales = quantise("xs%d" % s, shared_words[s][:].bitcast(BF16), T, tag, scale_tag)
+            codes, scales = quantise("xs%d" % s, shared_woven[s][:].bitcast(BF16), T)
             for b in range(T // P):
                 first_layer(s, E, SLOTS // P + b, codes, scales, b * P)
-        ys = y_banks[len(routed) % 2]
 
         picked = [tile("picked%d" % r, [P, T], F32) for r in range(TOP)]
         for r in range(TOP):
             nc.vector.tensor_tensor(picked[r][:], y_all[:].indirect(pos_t[r][:]), gate_t[:, r, :], MULT)
-        shared_cols = [h_cols[0], tile("shared_cols", [P, 4 * C], BF16)]
+
+        ys = y_banks[0]
+        shared_cols = [h_cols, tile("shared_cols", [P, 4 * C], BF16)]
         for half in range(2):
-            activate(len(routed) + half)
-            second_layer(len(routed) + half, shared_cols[half], ys[:, half * C : (half + 1) * C])
+            activate(E + half)
+            second_layer(E + half, shared_cols[half], ys[:, half * C : (half + 1) * C])
+
         sum2 = tile("sum2", [P, T], F32, "shared_cols")
         sum3 = tile("sum3", [P, T], F32)
         total = tile("total", [P, T], F32)

from contextlib import ExitStack

import concourse.mybir as mybir
from concourse.masks import make_identity

K, T, E, C, H, N = 1536, 512, 6, 256, 512, 128
TOP = 3
SLOTS = E * C
FLOPS = 2 * (SLOTS + T) * (K * H + H * N)

F32 = mybir.dt.float32
BF16 = mybir.dt.bfloat16
I32 = mybir.dt.int32
U32 = mybir.dt.uint32
U16 = mybir.dt.uint16
U8 = mybir.dt.uint8
FP8X4 = mybir.dt.float8_e4m3fn_x4
FP4X4 = mybir.dt.float4_e2m1fn_x4
GELU = mybir.ActivationFunctionType.Gelu_apprx_tanh
MULT = mybir.AluOpType.mult
ADD = mybir.AluOpType.add

P = 128
PASSES = K // 512
PIECES = 2 * PASSES
FIRST = 2
DEFERRED = 4
SCALE_GROUPS = ((0, 2), (2, 4), (4, 7))
GELU_AFTER = 2
TURN_AFTER = 3
KEEP_AFTER = 5
REUSE_AFTER = 4


def tile_moe_shr_mlp_gelu_kernel(
    tc, xT, w1_words, w1_scales, w2_words, w2_scales, gate, offs, pos1, pos2, pos3, out
):
    nc = tc.nc
    with ExitStack() as ctx:
        lists = ctx.enter_context(tc.tile_pool(name="lists", bufs=1))
        sb = ctx.enter_context(tc.tile_pool(name="sb", bufs=1))
        ps = ctx.enter_context(tc.psum_pool(name="ps", bufs=1))

        def tile(name, shape, dtype, after=None):
            return sb.tile(shape, dtype, name=name, tag=after or name, align_bytes=64)

        offs_t = lists.tile([P, SLOTS // 16], U16, name="offs_t")
        pos_t = [lists.tile([P, T // 16], U16, name="pos_t%d" % r) for r in range(TOP)]

        raw = [tile("raw%d" % j, [P, 2 * T], F32) for j in range(PIECES)]
        pairs = [tile("pairs%d" % s, [P, 4 * T], BF16) for s in range(PASSES)]
        w1_planes = {lo: tile("w1_planes%d" % lo, [P, (hi - lo) * PASSES, H], U8) for lo, hi in SCALE_GROUPS}
        w2 = tile("w2", [P, E + 1, 2 * N], U8)
        w2_planes = tile("w2_planes", [P, E + 1, N], U8)
        ident = tile("ident", [P, P], F32)
        warm_in = tile("warm_in", [P, 8], F32)
        warm_out = tile("warm_out", [P, 8], F32)

        nc.vector.memset(w1_planes[0][:].bitcast(I32), 0)
        nc.vector.memset(warm_in[:], 0.0)
        nc.scalar.activation(warm_out[:], warm_in[:], GELU)
        make_identity(nc, ident[:])
        nc.vector.memset(w1_planes[2][:].bitcast(I32), 0)
        nc.gpsimd.memset(w1_planes[4][:].bitcast(I32), 0)
        nc.gpsimd.memset(w2_planes[:].bitcast(I32), 0)

        x_rows = xT.rearrange("(s p u d) t -> s u p (d t)", s=PASSES, u=2, d=2)
        nc.sync.dma_start(raw[0][:], x_rows[0, 0])
        nc.sync.dma_start(offs_t[:], offs)
        for j in range(1, PIECES):
            nc.sync.dma_start(raw[j][:], x_rows[j // 2, j % 2])

        for j in range(PIECES):
            s, u = divmod(j, 2)
            rounded = pairs[s][:, 2 * u * T : 2 * (u + 1) * T].rearrange("p (t d) -> p t d", d=2)
            rows = raw[j][:].rearrange("p (d t) -> p t d", d=2)
            if j == 0:
                nc.vector.tensor_copy(rounded, rows)
            else:
                nc.scalar.copy(rounded, rows)

        def load_scales(planes, src):
            rows = src.rearrange("e s (q r) i -> r q (e s) i", r=4)
            for r in range(4):
                nc.sync.dma_start(planes[r:P:32, :, :].bitcast(I32), rows[r].bitcast(I32))

        w1 = {}

        def load_w1(lo, hi):
            words = tile("w1_%d" % lo, [P, (hi - lo) * PASSES, 2 * H], U8)
            nc.sync.dma_start(words[:].bitcast(I32), w1_words[lo:hi].rearrange("e s p b -> p (e s) b").bitcast(I32))
            for e in range(lo, hi):
                w1[e] = words[:, (e - lo) * PASSES : (e - lo + 1) * PASSES, :]

        w1_plane = {}
        for lo, hi in SCALE_GROUPS:
            load_w1(lo, min(hi, E))
            load_scales(w1_planes[lo], w1_scales[lo:hi])
            for e in range(lo, hi):
                w1_plane[e] = w1_planes[lo][:, (e - lo) * PASSES : (e - lo + 1) * PASSES, :]
        nc.sync.dma_start(w2[:].bitcast(I32), w2_words.rearrange("e s p b -> p (e s) b").bitcast(I32))
        load_scales(w2_planes, w2_scales)
        load_w1(E, E + 1)
        for r, pos in enumerate((pos1, pos2, pos3)):
            nc.sync.dma_start(pos_t[r][:], pos)
        gate_t = tile("gate_t", [P, TOP, T], F32)
        nc.sync.dma_start(gate_t[:], gate.rearrange("r p t -> p r t"))

        a_banks = [ps.tile([P, H], F32, name="a_bank%d" % i) for i in range(4)]
        t_banks = [ps.tile([P, 4 * P], F32, name="t_bank%d" % i) for i in range(2)]
        y_banks = [ps.tile([P, 2 * C], F32, name="y_bank%d" % i) for i in range(2)]
        h_rows = [tile("h_rows%d" % i, [P, 4 * C], BF16) for i in range((SLOTS + T) // P)]
        h_cols = tile("h_cols", [P, 4 * C], BF16)
        last_cols = tile("last_cols", [P, 4 * C], BF16)
        y_all = tile("y_all", [P, SLOTS], F32)

        def quantise(name, values, width, after=None):
            codes = tile("codes_" + name, [P, width], U32, after)
            scales = tile("scales_" + name, [P, width], U8)
            nc.vector.quantize_mx(out=codes[:].bitcast(FP8X4), scales=scales[:], in_=values)
            return codes, scales

        def first_layer(s, e, block, codes, scales, col):
            nc.tensor.matmul_mx(
                out=a_banks[block % 4][:],
                lhsT=codes[:, col : col + P].bitcast(FP8X4),
                lhsT_scale=scales[:, col : col + P],
                rhs=w1[e][:, s, :].bitcast(FP4X4),
                rhs_scale=w1_plane[e][:, s, :],
                start=(s == 0),
                stop=(s == PASSES - 1),
            )

        def activate(chunk):
            for b in range(2):
                block = 2 * chunk + b
                rows = h_rows[block][:, 0:H]
                nc.scalar.activation(
                    rows.rearrange("p (u m d) -> p u m d", u=2, d=2),
                    a_banks[block % 4][:].rearrange("p (m u d) -> p u m d", u=2, d=2),
                    GELU,
                )
                for u in range(2):
                    nc.tensor.transpose(
                        t_banks[chunk % 2][:, (2 * b + u) * P : (2 * b + u + 1) * P],
                        rows.bitcast(F32)[:, u * P : (u + 1) * P],
                        ident[:],
                    )

        def turn_out(chunk, cols):
            nc.scalar.copy(
                cols.bitcast(F32).rearrange("p (b t u) -> p b t u", t=P, u=2),
                t_banks[chunk % 2][:].rearrange("p (b u t) -> p b t u", u=2, t=P),
            )

        def project(e, codes, scales, y_out):
            nc.tensor.matmul_mx(
                out=y_out,
                lhsT=w2[:, e, :].bitcast(FP4X4),
                lhsT_scale=w2_planes[:, e, :],
                rhs=codes.bitcast(FP8X4),
                rhs_scale=scales,
                start=True,
                stop=True,
            )

        def second_layer(chunk, cols, y_out):
            turn_out(chunk, cols[:])
            codes, scales = quantise("h%d" % chunk, cols[:], C)
            project(min(chunk, E), codes[:], scales[:], y_out)

        deferred_cols = tile("deferred_cols", [P, DEFERRED * 4 * C], BF16)
        last_woven = tile("last_woven", [P, 2 * C], U32)

        steps = [(e, s) for s in range(PASSES) for e in range(FIRST)]
        steps = steps + [(e, s) for e in range(FIRST, E) for s in range(PASSES)]
        last = len(steps) - 1
        done_at = {e: steps.index((e, PASSES - 1)) for e in range(E)}

        gathered = []
        for n in range(len(steps)):
            if n < FIRST * PASSES:
                gathered.append(tile("gathered%d" % n, [P, 2 * C], U32))
            else:
                gathered.append(gathered[1 if n == FIRST * PASSES else n - 2])

        def woven_buffer(n):
            for e in range(FIRST):
                if n == done_at[e] + REUSE_AFTER:
                    return h_rows[2 * e][:].bitcast(U32)
            if n == last:
                return last_woven[:]
            return raw[PIECES - 1 - n % 4 // 2][:].bitcast(U32)[:, (n % 2) * 2 * C : (n % 2 + 1) * 2 * C]

        for n in range(len(steps) + KEEP_AFTER):
            if n <= last:
                e, s = steps[n]
                for u in range(2):
                    window = pairs[s][:].bitcast(U32)[:, u * T : (u + 1) * T]
                    nc.vector.tensor_copy(
                        gathered[n][:, u * C : (u + 1) * C],
                        window.indirect(offs_t[:, e * C // 16 : (e + 1) * C // 16]),
                    )
                woven = woven_buffer(n)
                nc.scalar.copy(woven.rearrange("p (c u) -> p c u", u=2), gathered[n][:].rearrange("p (u c) -> p c u", u=2))
            for done in range(E):
                if n == done_at[done] + GELU_AFTER:
                    activate(done)
            if n <= last:
                codes, scales = quantise("x%d" % n, woven.bitcast(BF16), C)
                for b in range(2):
                    first_layer(s, e, 2 * e + b, codes, scales, b * P)
            for done in range(E):
                turn_at = done_at[max(done, FIRST - 1)] + TURN_AFTER
                if done < DEFERRED:
                    if n == turn_at:
                        turn_out(done, deferred_cols[:, done * 4 * C : (done + 1) * 4 * C])
                    continue
                y_bank = t_banks[done % 2][:, 0:C]
                if n == turn_at:
                    second_layer(done, last_cols if done == E - 1 else h_cols, y_bank)
                if n == done_at[done] + KEEP_AFTER:
                    nc.scalar.copy(y_all[:, done * C : (done + 1) * C], y_bank)
            if n == last + TURN_AFTER:
                codes, scales = quantise("deferred", deferred_cols[:], DEFERRED * C, "last_woven")
                for bank in range(DEFERRED // 2):
                    for d in (2 * bank, 2 * bank + 1):
                        cols = slice(d * C, (d + 1) * C)
                        project(d, codes[:, cols], scales[:, cols], y_banks[bank][:, (d % 2) * C : (d % 2 + 1) * C])
                    nc.scalar.copy(y_all[:, 2 * bank * C : (2 * bank + 2) * C], y_banks[bank][:])

        shared_woven = []
        for s, after in enumerate(("codes_x%d" % last, "scales_x%d" % last, "last_cols")):
            words = tile("shared%d" % s, [P, 2 * T], I32, after)
            nc.vector.tensor_copy(
                words[:].rearrange("p (c u) -> p c u", u=2),
                pairs[s][:].bitcast(I32).rearrange("p (u c) -> p c u", u=2),
            )
            shared_woven.append(words)
        for s in range(PASSES):
            codes, scales = quantise("xs%d" % s, shared_woven[s][:].bitcast(BF16), T)
            for b in range(T // P):
                first_layer(s, E, SLOTS // P + b, codes, scales, b * P)

        picked = [tile("picked%d" % r, [P, T], F32) for r in range(TOP)]
        for r in range(TOP):
            nc.vector.tensor_tensor(picked[r][:], y_all[:].indirect(pos_t[r][:]), gate_t[:, r, :], MULT)

        ys = y_banks[0]
        shared_cols = [h_cols, tile("shared_cols", [P, 4 * C], BF16)]
        for half in range(2):
            activate(E + half)
            second_layer(E + half, shared_cols[half], ys[:, half * C : (half + 1) * C])

        sum2 = tile("sum2", [P, T], F32, "shared_cols")
        sum3 = tile("sum3", [P, T], F32)
        total = tile("total", [P, T], F32)
        halves = [slice(0, C), slice(C, T)]
        for cols in halves:
            nc.vector.tensor_tensor(sum2[:, cols], picked[0][:, cols], picked[1][:, cols], ADD)
        for cols in halves:
            nc.vector.tensor_tensor(sum3[:, cols], sum2[:, cols], picked[2][:, cols], ADD)
        for cols in halves:
            nc.vector.tensor_tensor(total[:, cols], sum3[:, cols], ys[:, cols], ADD)
            nc.sync.dma_start(out[:, cols], total[:, cols])
